import numpy as np
import ml_dtypes

BF16 = ml_dtypes.bfloat16


def bf(x):
    return np.asarray(x, np.float32).astype(BF16)


def f32(x):
    return np.asarray(x, np.float32)


def f64(x):
    return np.asarray(x).astype(np.float64)


def striped(idx):
    return np.concatenate([l.reshape(-1, 16).T for l in idx])


def rows(idx, k):
    return np.tile(np.repeat(idx, 16, axis=0), (k // (16 * 8), 1))


def look(tab, idx):
    return np.take_along_axis(f64(tab), rows(idx, len(tab)), axis=1)


K, S, D, V, N, M = 512, 2048, 1, 1024, 1024, 512


def setup_inputs():
    return {"tab": bf(0.7 * np.random.standard_normal((D, K, S))), "base": bf(np.random.standard_normal((K, V))), "w": bf(np.random.standard_normal((K, M)) / np.sqrt(K)), "b": f32(0.5 * np.random.standard_normal((M, 1))), "offs": striped(np.random.randint(0, S, (8, N)))}


def reference(tab, base, w, b, offs):
    idx = np.stack([g.T.reshape(-1) for g in np.split(offs, 8)])
    x = f64(base) + sum(look(tab[d], idx[:, d * V:(d + 1) * V]) for d in range(D))
    y = f64(w).T @ x
    return np.maximum(y + f64(b), 0.0)

@@ -1,0 +1,62 @@
+import concourse.mybir as mybir
+
+P = 128
+PIECE = 512
+GROUP = 16
+
+BF16, F32, U16 = mybir.dt.bfloat16, mybir.dt.float32, mybir.dt.uint16
+ADD, MAX = mybir.AluOpType.add, mybir.AluOpType.max
+RELU = mybir.ActivationFunctionType.Relu
+
+FLOPS = 2 * 512 * 512 * 1024
+
+
+def tile_lookup_res_add_relu_kernel(tc, tab, base, w, b, offs, out):
+    nc = tc.nc
+    rows, codewords = tab.shape[1], tab.shape[2]
+    n, m = base.shape[1], w.shape[1]
+    row_blocks, out_blocks, pieces = rows // P, m // P, n // PIECE
+
+    bias_rows = b.rearrange("(p j) one -> p (j one)", j=out_blocks)
+    out_rows = out.rearrange("(p j) n -> p j n", j=out_blocks)
+
+    early, late = range(row_blocks // 2), range(row_blocks // 2, row_blocks)
+    steps = [(k, c) for k in early for c in range(pieces)] + [(k, c) for c in range(pieces) for k in late]
+
+    with (
+        tc.tile_pool(name="held", bufs=1) as held,
+        tc.psum_pool(name="psum", bufs=1) as psum,
+    ):
+        offsets = held.tile([P, n // GROUP], U16, name="offsets")
+        bias = held.tile([P, out_blocks], F32, name="bias")
+        window = [held.tile([P, codewords], BF16, name=f"window{k}") for k in range(row_blocks)]
+        weights = [held.tile([P, m], BF16, name=f"weights{k}") for k in range(row_blocks)]
+        addend = {s: held.tile([P, PIECE], BF16, name=f"addend{s[0]}_{s[1]}") for s in steps}
+        x = {s: held.tile([P, PIECE], BF16, name=f"x{s[0]}_{s[1]}") for s in steps}
+        sums = [[psum.tile([P, PIECE], F32, name=f"sums{c}_{j}") for j in range(out_blocks)] for c in range(pieces)]
+
+        nc.sync.dma_start(offsets[:], offs)
+        for k, c in steps:
+            block = slice(k * P, (k + 1) * P)
+            if c == 0:
+                nc.sync.dma_start(window[k][:], tab[0, block, :])
+            nc.sync.dma_start(addend[k, c][:], base[block, c * PIECE:(c + 1) * PIECE])
+            if c == 0:
+                nc.sync.dma_start(weights[k][:], w[block, :])
+        nc.sync.dma_start(bias[:], bias_rows)
+
+        for k, c in steps:
+            entries = offsets[:, c * PIECE // GROUP:(c + 1) * PIECE // GROUP]
+            nc.vector.tensor_tensor(x[k, c][:], window[k][:].indirect(entries), addend[k, c][:], ADD)
+            for j in range(out_blocks):
+                nc.tensor.matmul(sums[c][j][:], weights[k][:, j::out_blocks], x[k, c][:],
+                                 start=(k == 0), stop=(k == row_blocks - 1))
+            if k < row_blocks - 1:
+                continue
+            for j in range(out_blocks):
+                result = held.tile([P, PIECE], F32, name=f"result{c}_{j}")
+                if c == pieces - 1 and j % 2 == 1:
+                    nc.vector.tensor_scalar(result[:], sums[c][j][:], bias[:, j:j + 1], 0.0, ADD, MAX)
+                else:
+                    nc.scalar.activation(result[:], sums[c][j][:], RELU, bias=bias[:, j:j + 1])
+                nc.sync.dma_start(out_rows[:, j, c * PIECE:(c + 1) * PIECE], result[:])

@@ -2,6 +2,7 @@ import concourse.mybir as mybir
 
 P = 128
 PIECE = 512
+WARMUP = 8
 GROUP = 16
 
 BF16, F32, U16 = mybir.dt.bfloat16, mybir.dt.float32, mybir.dt.uint16
@@ -35,6 +36,12 @@ def tile_lookup_res_add_relu_kernel(tc, tab, base, w, b, offs, out):
         x = {s: held.tile([P, PIECE], BF16, name=f"x{s[0]}_{s[1]}") for s in steps}
         sums = [[psum.tile([P, PIECE], F32, name=f"sums{c}_{j}") for j in range(out_blocks)] for c in range(pieces)]
 
+        zeros = held.tile([P, PIECE], BF16, name="zeros")
+        nc.vector.memset(zeros[:], 0.0)
+        for warm in range(WARMUP):
+            nc.tensor.matmul(sums[-1][-1][:], zeros[:, :P], zeros[:], start=True, stop=True)
+
+        nc.scalar.dma_start(bias[:], bias_rows)
         nc.sync.dma_start(offsets[:], offs)
         for k, c in steps:
             block = slice(k * P, (k + 1) * P)
@@ -43,7 +50,6 @@ def tile_lookup_res_add_relu_kernel(tc, tab, base, w, b, offs, out):
             nc.sync.dma_start(addend[k, c][:], base[block, c * PIECE:(c + 1) * PIECE])
             if c == 0:
                 nc.sync.dma_start(weights[k][:], w[block, :])
-        nc.sync.dma_start(bias[:], bias_rows)
 
         for k, c in steps:
             entries = offsets[:, c * PIECE // GROUP:(c + 1) * PIECE // GROUP]

@@ -2,7 +2,8 @@ import concourse.mybir as mybir
 
 P = 128
 PIECE = 512
-WARMUP = 8
+WARMUP_LOAD = 6
+WARMUP_LOOKUP = 3
 GROUP = 16
 
 BF16, F32, U16 = mybir.dt.bfloat16, mybir.dt.float32, mybir.dt.uint16
@@ -36,20 +37,34 @@ def tile_lookup_res_add_relu_kernel(tc, tab, base, w, b, offs, out):
         x = {s: held.tile([P, PIECE], BF16, name=f"x{s[0]}_{s[1]}") for s in steps}
         sums = [[psum.tile([P, PIECE], F32, name=f"sums{c}_{j}") for j in range(out_blocks)] for c in range(pieces)]
 
-        zeros = held.tile([P, PIECE], BF16, name="zeros")
-        nc.vector.memset(zeros[:], 0.0)
-        for warm in range(WARMUP):
-            nc.tensor.matmul(sums[-1][-1][:], zeros[:, :P], zeros[:], start=True, stop=True)
+        def load_window(k):
+            nc.sync.dma_start(window[k][:], tab[0, k * P:(k + 1) * P, :])
+
+        def load_weights(k):
+            nc.sync.dma_start(weights[k][:], w[k * P:(k + 1) * P, :])
+
+        def load_addend(k, c):
+            nc.sync.dma_start(addend[k, c][:], base[k * P:(k + 1) * P, c * PIECE:(c + 1) * PIECE])
 
         nc.scalar.dma_start(bias[:], bias_rows)
         nc.sync.dma_start(offsets[:], offs)
-        for k, c in steps:
-            block = slice(k * P, (k + 1) * P)
-            if c == 0:
-                nc.sync.dma_start(window[k][:], tab[0, block, :])
-            nc.sync.dma_start(addend[k, c][:], base[block, c * PIECE:(c + 1) * PIECE])
-            if c == 0:
-                nc.sync.dma_start(weights[k][:], w[block, :])
+        for k in early:
+            load_window(k)
+            load_addend(k, 0)
+            load_weights(k)
+            load_addend(k, 1)
+        for k in late:
+            load_window(k)
+            load_addend(k, 0)
+        for k in late:
+            load_weights(k)
+        for k in late:
+            load_addend(k, 1)
+
+        zeros = held.tile([P, PIECE], BF16, name="zeros")
+        nc.vector.memset(zeros[:], 0.0)
+        for moving in [zeros] * WARMUP_LOAD + [addend[steps[0]]] * WARMUP_LOOKUP:
+            nc.tensor.matmul(sums[-1][-1][:], zeros[:, :P], moving[:], start=True, stop=True)
 
         for k, c in steps:
             entries = offsets[:, c * PIECE // GROUP:(c + 1) * PIECE // GROUP]
@@ -61,7 +76,7 @@ def tile_lookup_res_add_relu_kernel(tc, tab, base, w, b, offs, out):
                 continue
             for j in range(out_blocks):
                 result = held.tile([P, PIECE], F32, name=f"result{c}_{j}")
-                if c == pieces - 1 and j % 2 == 1:
+                if c == pieces - 1 and j % 2 == 0:
                     nc.vector.tensor_scalar(result[:], sums[c][j][:], bias[:, j:j + 1], 0.0, ADD, MAX)
                 else:
                     nc.scalar.activation(result[:], sums[c][j][:], RELU, bias=bias[:, j:j + 1])

@@ -47,9 +47,10 @@ def tile_lookup_res_add_relu_kernel(tc, tab, base, w, b, offs, out):
             nc.sync.dma_start(addend[k, c][:], base[k * P:(k + 1) * P, c * PIECE:(c + 1) * PIECE])
 
         nc.scalar.dma_start(bias[:], bias_rows)
-        nc.sync.dma_start(offsets[:], offs)
         for k in early:
             load_window(k)
+            if k == 0:
+                nc.sync.dma_start(offsets[:], offs)
             load_addend(k, 0)
             load_weights(k)
             load_addend(k, 1)
@@ -76,8 +77,11 @@ def tile_lookup_res_add_relu_kernel(tc, tab, base, w, b, offs, out):
                 continue
             for j in range(out_blocks):
                 result = held.tile([P, PIECE], F32, name=f"result{c}_{j}")
-                if c == pieces - 1 and j % 2 == 0:
-                    nc.vector.tensor_scalar(result[:], sums[c][j][:], bias[:, j:j + 1], 0.0, ADD, MAX)
-                else:
-                    nc.scalar.activation(result[:], sums[c][j][:], RELU, bias=bias[:, j:j + 1])
-                nc.sync.dma_start(out_rows[:, j, c * PIECE:(c + 1) * PIECE], result[:])
+                width = PIECE // 2 if j == 0 else PIECE
+                for first in range(0, PIECE, width):
+                    cols = slice(first, first + width)
+                    if c == pieces - 1 and j % 2 == 0:
+                        nc.vector.tensor_scalar(result[:, cols], sums[c][j][:, cols], bias[:, j:j + 1], 0.0, ADD, MAX)
+                    else:
+                        nc.scalar.activation(result[:, cols], sums[c][j][:, cols], RELU, bias=bias[:, j:j + 1])
+                    nc.sync.dma_start(out_rows[:, j, c * PIECE + first:c * PIECE + first + width], result[:, cols])

@@ -3,7 +3,7 @@ import concourse.mybir as mybir
 P = 128
 PIECE = 512
 WARMUP_LOAD = 6
-WARMUP_LOOKUP = 3
+WARMUP_LOOKUP = 2
 GROUP = 16
 
 BF16, F32, U16 = mybir.dt.bfloat16, mybir.dt.float32, mybir.dt.uint16
@@ -44,9 +44,9 @@ def tile_lookup_res_add_relu_kernel(tc, tab, base, w, b, offs, out):
             nc.sync.dma_start(weights[k][:], w[k * P:(k + 1) * P, :])
 
         def load_addend(k, c):
-            nc.sync.dma_start(addend[k, c][:], base[k * P:(k + 1) * P, c * PIECE:(c + 1) * PIECE])
+            queue = nc.scalar if (k, c) == steps[0] else nc.sync
+            queue.dma_start(addend[k, c][:], base[k * P:(k + 1) * P, c * PIECE:(c + 1) * PIECE])
 
-        nc.scalar.dma_start(bias[:], bias_rows)
         for k in early:
             load_window(k)
             if k == 0:
@@ -59,13 +59,16 @@ def tile_lookup_res_add_relu_kernel(tc, tab, base, w, b, offs, out):
             load_addend(k, 0)
         for k in late:
             load_weights(k)
+        nc.sync.dma_start(bias[:], bias_rows)
         for k in late:
             load_addend(k, 1)
 
         zeros = held.tile([P, PIECE], BF16, name="zeros")
         nc.vector.memset(zeros[:], 0.0)
-        for moving in [zeros] * WARMUP_LOAD + [addend[steps[0]]] * WARMUP_LOOKUP:
+        for moving in [zeros] * WARMUP_LOAD + [weights[0]] * WARMUP_LOOKUP:
             nc.tensor.matmul(sums[-1][-1][:], zeros[:, :P], moving[:], start=True, stop=True)
+        unused = held.tile([P, GROUP], F32, name="unused")
+        nc.scalar.activation(unused[:], zeros[:, :GROUP], RELU)
 
         for k, c in steps:
             entries = offsets[:, c * PIECE // GROUP:(c + 1) * PIECE // GROUP]

import concourse.mybir as mybir

P = 128
PIECE = 512
WARMUP_LOAD = 6
WARMUP_LOOKUP = 2
GROUP = 16

BF16, F32, U16 = mybir.dt.bfloat16, mybir.dt.float32, mybir.dt.uint16
ADD, MAX = mybir.AluOpType.add, mybir.AluOpType.max
RELU = mybir.ActivationFunctionType.Relu

FLOPS = 2 * 512 * 512 * 1024


def tile_lookup_res_add_relu_kernel(tc, tab, base, w, b, offs, out):
    nc = tc.nc
    rows, codewords = tab.shape[1], tab.shape[2]
    n, m = base.shape[1], w.shape[1]
    row_blocks, out_blocks, pieces = rows // P, m // P, n // PIECE

    bias_rows = b.rearrange("(p j) one -> p (j one)", j=out_blocks)
    out_rows = out.rearrange("(p j) n -> p j n", j=out_blocks)

    early, late = range(row_blocks // 2), range(row_blocks // 2, row_blocks)
    steps = [(k, c) for k in early for c in range(pieces)] + [(k, c) for c in range(pieces) for k in late]

    with (
        tc.tile_pool(name="held", bufs=1) as held,
        tc.psum_pool(name="psum", bufs=1) as psum,
    ):
        offsets = held.tile([P, n // GROUP], U16, name="offsets")
        bias = held.tile([P, out_blocks], F32, name="bias")
        window = [held.tile([P, codewords], BF16, name=f"window{k}") for k in range(row_blocks)]
        weights = [held.tile([P, m], BF16, name=f"weights{k}") for k in range(row_blocks)]
        addend = {s: held.tile([P, PIECE], BF16, name=f"addend{s[0]}_{s[1]}") for s in steps}
        x = {s: held.tile([P, PIECE], BF16, name=f"x{s[0]}_{s[1]}") for s in steps}
        sums = [[psum.tile([P, PIECE], F32, name=f"sums{c}_{j}") for j in range(out_blocks)] for c in range(pieces)]

        def load_window(k):
            nc.sync.dma_start(window[k][:], tab[0, k * P:(k + 1) * P, :])

        def load_weights(k):
            nc.sync.dma_start(weights[k][:], w[k * P:(k + 1) * P, :])

        def load_addend(k, c):
            queue = nc.scalar if (k, c) == steps[0] else nc.sync
            queue.dma_start(addend[k, c][:], base[k * P:(k + 1) * P, c * PIECE:(c + 1) * PIECE])

        for k in early:
            load_window(k)
            if k == 0:
                nc.sync.dma_start(offsets[:], offs)
            load_addend(k, 0)
            load_weights(k)
            load_addend(k, 1)
        for k in late:
            load_window(k)
            load_addend(k, 0)
        for k in late:
            load_weights(k)
        nc.sync.dma_start(bias[:], bias_rows)
        for k in late:
            load_addend(k, 1)

        zeros = held.tile([P, PIECE], BF16, name="zeros")
        nc.vector.memset(zeros[:], 0.0)
        for moving in [zeros] * WARMUP_LOAD + [weights[0]] * WARMUP_LOOKUP:
            nc.tensor.matmul(sums[-1][-1][:], zeros[:, :P], moving[:], start=True, stop=True)
        unused = held.tile([P, GROUP], F32, name="unused")
        nc.scalar.activation(unused[:], zeros[:, :GROUP], RELU)

        for k, c in steps:
            entries = offsets[:, c * PIECE // GROUP:(c + 1) * PIECE // GROUP]
            nc.vector.tensor_tensor(x[k, c][:], window[k][:].indirect(entries), addend[k, c][:], ADD)
            for j in range(out_blocks):
                nc.tensor.matmul(sums[c][j][:], weights[k][:, j::out_blocks], x[k, c][:],
                                 start=(k == 0), stop=(k == row_blocks - 1))
            if k < row_blocks - 1:
                continue
            for j in range(out_blocks):
                result = held.tile([P, PIECE], F32, name=f"result{c}_{j}")
                width = PIECE // 2 if j == 0 else PIECE
                for first in range(0, PIECE, width):
                    cols = slice(first, first + width)
                    if c == pieces - 1 and j % 2 == 0:
                        nc.vector.tensor_scalar(result[:, cols], sums[c][j][:, cols], bias[:, j:j + 1], 0.0, ADD, MAX)
                    else:
                        nc.scalar.activation(result[:, cols], sums[c][j][:, cols], RELU, bias=bias[:, j:j + 1])
                    nc.sync.dma_start(out_rows[:, j, c * PIECE + first:c * PIECE + first + width], result[:, cols])
